import numpy as np
import ml_dtypes


def mxq(x, axis, fmt="e4m3"):
    dtype, down = {"e4m3": (ml_dtypes.float8_e4m3fn, 7), "e5m2": (ml_dtypes.float8_e5m2, 14)}[fmt]
    v = np.moveaxis(np.asarray(x, np.float32).astype(ml_dtypes.bfloat16).astype(np.float64), axis, -1)
    blocks = v.reshape(v.shape[:-1] + (-1, 32))
    amax = np.abs(blocks).max(-1, keepdims=True)
    byte = np.maximum(np.where(amax > 0, np.frexp(amax)[1] - 1 + 127, 0) - down, 1)
    scale = np.exp2(byte - 127.0)
    codes = (blocks / scale).astype(np.float32).astype(dtype).astype(np.float64)
    return np.moveaxis((codes * scale).reshape(v.shape), -1, axis)


WIDE = False


def mx_kscale(k):
    if not WIDE:
        return np.ones(k)
    levels = np.array([10, -10, 5, -5, 0])
    if k % 512:
        return np.exp2(np.random.permutation(np.resize(levels, k // 32))).repeat(32)
    a = np.empty((k // 512, 16))
    for p in range(k // 512):
        a[p, :8] = np.random.permutation(np.resize(levels, 8))
        for g in range(8):
            far = levels[np.abs(levels - a[p, g]) >= 10]
            a[p, g + 8] = far[np.random.randint(len(far))]
    return np.exp2(a.ravel()).repeat(32)


def f64(x):
    return np.asarray(x).astype(np.float64)


def striped(idx):
    return np.tile(idx.reshape(-1, 16).T, (8, 1)).astype(np.uint16)


def unstriped(offs):
    return offs[:16].T.reshape(-1).astype(np.int64)


def striped8(idx):
    return np.concatenate([x.reshape(-1, 16).T for x in idx]).astype(np.uint16)


def runs(offs, k):
    lists = np.stack([offs[16 * r : 16 * r + 16].T.reshape(-1) for r in range(8)]).astype(np.int64)
    return lists[np.arange(k) % 512 // 64]


def pack_weight(w):
    k, n = w.shape
    w = f64(np.asarray(w, np.float32).astype(ml_dtypes.bfloat16)).reshape(k // 32, 32, n)
    amax = np.abs(w).max(1)
    byte = np.clip(np.where(amax > 0, np.frexp(amax)[1] - 1 + 127 - 7, 1), 1, 254)
    scaled = (w * np.exp2(127.0 - byte)[:, None, :]).reshape(k, n).astype(np.float32)
    words = np.ascontiguousarray(scaled.reshape(k // 512, 128, 4, n).transpose(0, 1, 3, 2)).astype(ml_dtypes.float8_e4m3fn).view(np.uint8)
    return words, np.ascontiguousarray(byte.astype(np.uint8).reshape(k // 512, 16, n))


def unpack_weight(words, scales):
    g, p, n, _ = words.shape
    vals = np.ascontiguousarray(words).view(ml_dtypes.float8_e4m3fn).astype(np.float64) * np.repeat(np.exp2(scales.astype(np.float64) - 127.0), 8, axis=1)[..., None]
    return vals.transpose(0, 1, 3, 2).reshape(g * 512, n)


def sigmoid(v):
    return 1.0 / (1.0 + np.exp(-np.maximum(v, -700.0)))

def planes(y):
    n, m = y.shape
    v = y.astype(np.float32).astype(ml_dtypes.bfloat16).astype(np.float64).reshape(n // 32, 32, m)
    top = np.abs(v).max(1)
    byte = np.clip(np.where(top > 0, np.frexp(top)[1] - 1 + 127 - 7, 1), 1, 254)
    codes = (v * np.exp2(127.0 - byte)[:, None, :]).reshape(n, m).astype(np.float32).astype(ml_dtypes.float8_e4m3fn).view(np.uint8)
    words = codes.reshape(n // 512, 128, 4, m).transpose(0, 1, 3, 2)
    return np.ascontiguousarray(words), np.ascontiguousarray(byte.astype(np.uint8).reshape(n // 512, 16, m))


K, T, S, V, H = 512, 2048, 512, 512, 512


def setup_inputs():
    n = np.random.standard_normal
    s = mx_kscale(K)[:, None]
    u = mx_kscale(S)
    packed_xT = pack_weight(n((K, T)) * s)
    packed_w1 = pack_weight(n((K, H)) / np.sqrt(K) / s)
    packed_w2 = pack_weight(n((K, H)) / np.sqrt(K) / s)
    return {
        "x_words": packed_xT[0],
        "x_scales": packed_xT[1],
        "w1_words": packed_w1[0],
        "w1_scales": packed_w1[1],
        "w2_words": packed_w2[0],
        "w2_scales": packed_w2[1],
        "ga": (np.random.uniform(0.5, 1.5, (H, 1)) * u[:, None]).astype(np.float32),
        "gb": (np.random.uniform(0.5, 1.5, (H, 1)) / u[:, None]).astype(np.float32),
        "offs": striped(np.random.permutation(T)[:S]),
        "two": striped(np.random.permutation(T)[:V]),
        "n1": striped8(np.stack([np.random.permutation(S) for _ in range(8)])),
        "n2": striped8(np.stack([np.random.permutation(S) for _ in range(8)])),
        "nq": striped8(np.stack([np.random.permutation(V) for _ in range(8)])),
        "cq": striped8(np.stack([np.random.permutation(V) for _ in range(8)])),
    }


def reference(x_words, x_scales, w1_words, w1_scales, w2_words, w2_scales, ga, gb, offs, two, n1, n2, nq, cq):
    xq = unpack_weight(x_words, x_scales)[:, unstriped(offs)]
    a = unpack_weight(w1_words, w1_scales).T @ xq
    k1 = a[np.arange(H)[:, None], runs(n1, H)]
    k2 = a[np.arange(H)[:, None], runs(n2, H)]
    z = f64(ga) * (np.maximum(np.minimum(a, k1), np.minimum(np.maximum(a, k1), k2)))
    x_two = unpack_weight(x_words, x_scales)[:, unstriped(two)]
    b = unpack_weight(w2_words, w2_scales).T @ x_two
    z2 = f64(gb) * (b * (sigmoid(b[np.arange(H)[:, None], runs(nq, H)])))
    s = 0.0625 * ((mxq(z, 0, "e4m3").T @ mxq(z2, 0, "e4m3")))
    out_0 = s - (0.5 * (s[np.arange(S)[:, None], runs(cq, S)]))
    return (out_0,) + planes(out_0)

@@ -1,0 +1,227 @@
+from contextlib import ExitStack
+
+import concourse.mybir as mybir
+
+F32 = mybir.dt.float32
+BF16 = mybir.dt.bfloat16
+I32 = mybir.dt.int32
+U32 = mybir.dt.uint32
+U16 = mybir.dt.uint16
+U8 = mybir.dt.uint8
+FP8X4 = mybir.dt.float8_e4m3fn_x4
+ALU = mybir.AluOpType
+ACT = mybir.ActivationFunctionType
+
+P = 128
+PACK = 4
+T = 2048
+N = 512
+HALF = N // 2
+LIST_COLS = N // 16
+FLOPS = 3 * 2 * 512 * 512 * 512
+
+
+def tile_picked_keymed_none_po_kernel(
+    tc, x_words, x_scales, w1_words, w1_scales, w2_words, w2_scales, ga, gb, offs, two, n1, n2, nq, cq, out_0, out_1, out_2
+):
+    nc = tc.nc
+    with ExitStack() as ctx:
+        lists = ctx.enter_context(tc.tile_pool(name="lists", bufs=1))
+        sb = ctx.enter_context(tc.tile_pool(name="sb", bufs=1))
+        psum = ctx.enter_context(tc.psum_pool(name="psum", bufs=1))
+
+        def tile(name, shape, dtype, tag=None):
+            return sb.tile(shape, dtype, name=name, tag=tag or name, align_bytes=64)
+
+        def load_list(name, src):
+            held = lists.tile([P, LIST_COLS], U16, name=name)
+            nc.sync.dma_start(held[:], src)
+            return held
+
+        def load_words(name, src, width):
+            held = tile(name, [P, width], U32)
+            nc.sync.dma_start(held[:].bitcast(I32), src[0].rearrange("p n t -> p (n t)").bitcast(I32))
+            return held
+
+        def load_scales(queue, held, src, quadrants=range(4)):
+            for q in quadrants:
+                queue.dma_start(held[32 * q : 32 * q + 4, :].bitcast(I32), src[0, 4 * q : 4 * q + 4, :].bitcast(I32))
+
+        def half_of(held, h):
+            return held[:, h * (LIST_COLS // 2) : (h + 1) * (LIST_COLS // 2)]
+
+        def cols(h):
+            return slice(h * HALF, (h + 1) * HALF)
+
+        w1s = tile("w1s", [P, N], U8)
+        w2s = tile("w2s", [P, N], U8)
+        xs = tile("xs", [P, T], U8)
+        nc.vector.memset(xs[:].bitcast(I32), 0)
+        nc.gpsimd.memset(w2s[:].bitcast(I32), 0)
+        nc.vector.memset(w1s[:].bitcast(I32), 0)
+
+        two_l = load_list("two_l", two)
+        xw = load_words("xw", x_words, T)
+        load_scales(nc.sync, xs, x_scales)
+        w2w = load_words("w2w", w2_words, N)
+        load_scales(nc.sync, w2s, w2_scales, range(2))
+        load_scales(nc.gpsimd, w2s, w2_scales, range(2, 4))
+        ga_t = tile("ga_t", [P, PACK], F32)
+        gb_t = tile("gb_t", [P, PACK], F32)
+        nc.gpsimd.dma_start(ga_t[:], ga.rearrange("(p t) o -> p (t o)", t=PACK))
+        nc.gpsimd.dma_start(gb_t[:], gb.rearrange("(p t) o -> p (t o)", t=PACK))
+        offs_l = load_list("offs_l", offs)
+        w1w = load_words("w1w", w1_words, N)
+        load_scales(nc.sync, w1s, w1_scales)
+        nq_l = load_list("nq_l", nq)
+        n1_l = load_list("n1_l", n1)
+        n2_l = load_list("n2_l", n2)
+        cq_l = load_list("cq_l", cq)
+
+        def deal(copy, name, src, dtype):
+            dealt = tile(name, [P, N], dtype)
+            copy(dealt[:].rearrange("p (t m) -> p m t", t=PACK), src[:].rearrange("p (m t) -> p m t", t=PACK))
+            return dealt
+
+        def pick(name, window, offsets, dtype):
+            picked = tile(name, [P, N], dtype)
+            nc.vector.tensor_copy(picked[:], window[:].indirect(offsets[:]))
+            return picked
+
+        def product(out, lw, ls, t, rw, rs):
+            m = slice(t * P, (t + 1) * P)
+            nc.tensor.matmul_mx(out, lhsT=lw[:, m].bitcast(FP8X4), lhsT_scale=ls[:, m], rhs=rw.bitcast(FP8X4), rhs_scale=rs, start=True, stop=True)
+
+        w2s_d = deal(nc.vector.tensor_copy, "w2s_d", w2s, U8)
+        w2w_d = deal(nc.scalar.copy, "w2w_d", w2w, U32)
+        x2w = pick("x2w", xw, two_l, U32)
+        x2s = pick("x2s", xs, two_l, U8)
+        b_ps = [psum.tile([P, N], F32, name=f"b_ps{t}", tag=f"bank{4 + t}") for t in range(PACK)]
+        for t in range(PACK):
+            product(b_ps[t][:], w2w_d, w2s_d, t, x2w[:], x2s[:])
+        w1w_d = deal(nc.scalar.copy, "w1w_d", w1w, U32)
+        x1w = pick("x1w", xw, offs_l, U32)
+        x1s = pick("x1s", xs, offs_l, U8)
+        w1s_d = deal(nc.vector.tensor_copy, "w1s_d", w1s, U8)
+        a_ps = [psum.tile([P, N], F32, name=f"a_ps{t}", tag=f"bank{t}") for t in range(PACK)]
+        for t in range(PACK):
+            product(a_ps[t][:], w1w_d, w1s_d, t, x1w[:], x1s[:])
+
+        a_sb = [tile(f"a_sb{t}", [P, N], F32) for t in range(PACK)]
+        b_sb = [tile(f"b_sb{t}", [P, N], F32) for t in range(PACK)]
+        k1 = [tile(f"k1_{t}", [P, N], BF16) for t in range(PACK)]
+        k2 = [tile(f"k2_{t}", [P, N], BF16) for t in range(PACK)]
+        lo = tile("lo", [P, PACK, N], BF16)
+        hi = tile("hi", [P, PACK, N], BF16)
+        mid = tile("mid", [P, PACK, N], BF16)
+        z = tile("z", [P, PACK, N], BF16)
+        sig = {}
+        z2 = tile("z2", [P, PACK, N], BF16)
+        z_in = tile("z_in", [P, PACK * N], BF16)
+        z2_in = tile("z2_in", [P, PACK * N], BF16)
+        zw = tile("zw", [P, N], U32)
+        zs = tile("zs", [P, N], U8)
+        z2w = tile("z2w", [P, N], U32)
+        z2s = tile("z2s", [P, N], U8)
+
+        def leave_a(t):
+            nc.scalar.activation(a_sb[t][:], a_ps[t][:], ACT.Copy, scale=ga_t[:, t : t + 1])
+
+        def fetch_scalar(out, window, held, h):
+            nc.scalar.activation(out, window[:].indirect(half_of(held, h)), ACT.Copy)
+
+        def fetch_vector(out, window, held, h):
+            nc.vector.tensor_copy(out, window[:].indirect(half_of(held, h)))
+
+        def keys(t, on_vector):
+            for n, (dst, held, h) in enumerate([(k1, n1_l, 0), (k2, n2_l, 0), (k1, n1_l, 1), (k2, n2_l, 1)]):
+                fetch = fetch_vector if n < on_vector else fetch_scalar
+                fetch(dst[t][:, cols(h)], a_sb[t], held, h)
+
+        def median(t):
+            nc.vector.tensor_tensor(hi[:, t, :], k1[t][:], k2[t][:], ALU.max)
+            nc.vector.tensor_tensor(lo[:, t, :], k1[t][:], k2[t][:], ALU.min)
+            nc.vector.tensor_tensor(mid[:, t, :], a_sb[t][:], hi[:, t, :], ALU.min)
+            nc.vector.tensor_tensor(z[:, t, :], lo[:, t, :], mid[:, t, :], ALU.max)
+
+        def gate(t, h, fetch, tag):
+            sig[t, h] = tile(f"sig{t}{h}", [P, HALF], F32, tag)
+            fetch(sig[t, h][:], b_sb[t], nq_l, h)
+
+        def weave(dst, src):
+            nc.vector.tensor_copy(dst.rearrange("p (c i t) -> p c t i", i=4, t=PACK), src.rearrange("p t (c i) -> p c t i", i=4))
+
+        def queries(h):
+            for t in range(PACK):
+                nc.vector.scalar_tensor_tensor(z2[:, t, cols(h)], b_ps[t][:, cols(h)], gb_t[:, t : t + 1], sig[t, h][:], ALU.mult, ALU.mult)
+            wide = slice(h * PACK * HALF, (h + 1) * PACK * HALF)
+            weave(z2_in[:, wide], z2[:, :, cols(h)])
+            nc.vector.quantize_mx(z2w[:, cols(h)].bitcast(FP8X4), z2s[:, cols(h)], z2_in[:, wide])
+
+        for t in range(PACK):
+            nc.scalar.activation(b_sb[t][:], b_ps[t][:], ACT.Sigmoid)
+        gate(3, 0, fetch_scalar, None)
+        leave_a(0)
+        keys(0, 0)
+        for t in range(PACK - 1):
+            gate(t, 0, fetch_vector, None)
+        leave_a(1)
+        keys(1, 0)
+        queries(0)
+        median(0)
+        leave_a(2)
+        leave_a(3)
+        median(1)
+        keys(2, 2)
+        keys(3, 1)
+        median(2)
+        for t in range(PACK):
+            gate(t, 1, fetch_scalar, f"k{1 + t % 2}_{t // 2}")
+        median(3)
+        nc.vector.tensor_copy(z_in[:].rearrange("p (u m t) -> p m t u", u=PACK, t=PACK), z[:].rearrange("p t (m u) -> p m t u", u=PACK))
+        nc.vector.quantize_mx(zw[:].bitcast(FP8X4), zs[:], z_in[:])
+
+        s_ps = [[psum.tile([P, 2, HALF], F32, name=f"s_ps{h}{u}", tag=f"bank{2 * h + u}") for u in range(2)] for h in range(2)]
+        s_sb = [tile(f"s_sb{t}", [P, N], F32) for t in range(PACK)]
+        got = tile("got", [P, PACK, N], F32)
+        res = tile("res", [P, PACK, N], F32)
+        res_in = tile("res_in", [P, PACK * N], BF16)
+        ow = tile("ow", [P, N], U32)
+        osc = tile("osc", [P, N], U8)
+
+        def scores(h):
+            for t in range(PACK):
+                product(s_ps[h][t // 2][:, t % 2, :], zw, zs, t, z2w[:, cols(h)], z2s[:, cols(h)])
+
+        def leave_s(t, h, on_vector):
+            src = s_ps[h][t // 2][:, t % 2, :]
+            if on_vector:
+                nc.vector.tensor_scalar(s_sb[t][:, cols(h)], src, -0.03125, None, ALU.mult)
+            else:
+                nc.scalar.activation(s_sb[t][:, cols(h)], src, ACT.Copy, scale=-0.03125)
+
+        scores(0)
+        for t in range(PACK):
+            leave_s(t, 0, False)
+        queries(1)
+        scores(1)
+        for t in range(PACK):
+            leave_s(t, 1, t >= 2)
+
+        out_rows = out_0.rearrange("(p t) v -> p t v", t=PACK)
+        out_words = out_1[0].rearrange("p n t -> p (n t)").bitcast(I32)
+        for h in range(2):
+            for u in range(2):
+                for t in (2 * u, 2 * u + 1):
+                    fetch = fetch_vector if h == 0 and t >= 2 else fetch_scalar
+                    fetch(got[:, t, cols(h)], s_sb[t], cq_l, h)
+                pair = slice(2 * u, 2 * u + 2)
+                nc.vector.scalar_tensor_tensor(res[:, pair, cols(h)], s_ps[h][u][:], 0.0625, got[:, pair, cols(h)], ALU.mult, ALU.add)
+                nc.sync.dma_start(out_rows[:, pair, cols(h)], res[:, pair, cols(h)])
+            wide = slice(h * PACK * HALF, (h + 1) * PACK * HALF)
+            weave(res_in[:, wide], res[:, :, cols(h)])
+            nc.vector.quantize_mx(ow[:, cols(h)].bitcast(FP8X4), osc[:, cols(h)], res_in[:, wide])
+            nc.sync.dma_start(out_words[:, cols(h)], ow[:, cols(h)].bitcast(I32))
+        for q in range(4):
+            queue = nc.scalar if q % 2 else nc.sync
+            queue.dma_start(out_2[0, 4 * q : 4 * q + 4, :].bitcast(I32), osc[32 * q : 32 * q + 4, :].bitcast(I32))

@@ -56,27 +56,31 @@ def tile_picked_keymed_none_po_kernel(
         w1s = tile("w1s", [P, N], U8)
         w2s = tile("w2s", [P, N], U8)
         xs = tile("xs", [P, T], U8)
-        nc.vector.memset(xs[:].bitcast(I32), 0)
-        nc.gpsimd.memset(w2s[:].bitcast(I32), 0)
-        nc.vector.memset(w1s[:].bitcast(I32), 0)
+        nc.gpsimd.memset(xs[:].bitcast(I32), 0)
+        nc.vector.memset(w2s[:].bitcast(I32), 0)
+        nc.gpsimd.memset(w1s[:].bitcast(I32), 0)
 
         two_l = load_list("two_l", two)
-        xw = load_words("xw", x_words, T)
+        offs_l = load_list("offs_l", offs)
         load_scales(nc.sync, xs, x_scales)
+        xw = load_words("xw", x_words, T)
         w2w = load_words("w2w", w2_words, N)
-        load_scales(nc.sync, w2s, w2_scales, range(2))
-        load_scales(nc.gpsimd, w2s, w2_scales, range(2, 4))
+        load_scales(nc.sync, w2s, w2_scales)
+        w1w = load_words("w1w", w1_words, N)
+        load_scales(nc.gpsimd, w1s, w1_scales)
+        nq_l = load_list("nq_l", nq)
         ga_t = tile("ga_t", [P, PACK], F32)
         gb_t = tile("gb_t", [P, PACK], F32)
-        nc.gpsimd.dma_start(ga_t[:], ga.rearrange("(p t) o -> p (t o)", t=PACK))
-        nc.gpsimd.dma_start(gb_t[:], gb.rearrange("(p t) o -> p (t o)", t=PACK))
-        offs_l = load_list("offs_l", offs)
-        w1w = load_words("w1w", w1_words, N)
-        load_scales(nc.sync, w1s, w1_scales)
-        nq_l = load_list("nq_l", nq)
+        nc.sync.dma_start(ga_t[:], ga.rearrange("(p t) o -> p (t o)", t=PACK))
         n1_l = load_list("n1_l", n1)
         n2_l = load_list("n2_l", n2)
+        nc.sync.dma_start(gb_t[:], gb.rearrange("(p t) o -> p (t o)", t=PACK))
         cq_l = load_list("cq_l", cq)
+
+        def deal_bytes(name, src):
+            dealt = tile(name, [P, N], U8)
+            nc.gpsimd.tensor_copy(dealt[:].rearrange("p (t m) -> p t m", t=PACK), src[:].rearrange("p (m t) -> p t m", t=PACK))
+            return dealt
 
         def deal(copy, name, src, dtype):
             dealt = tile(name, [P, N], dtype)
@@ -92,17 +96,17 @@ def tile_picked_keymed_none_po_kernel(
             m = slice(t * P, (t + 1) * P)
             nc.tensor.matmul_mx(out, lhsT=lw[:, m].bitcast(FP8X4), lhsT_scale=ls[:, m], rhs=rw.bitcast(FP8X4), rhs_scale=rs, start=True, stop=True)
 
-        w2s_d = deal(nc.vector.tensor_copy, "w2s_d", w2s, U8)
+        x2s = pick("x2s", xs, two_l, U8)
+        x1s = pick("x1s", xs, offs_l, U8)
+        w2s_d = deal_bytes("w2s_d", w2s)
         w2w_d = deal(nc.scalar.copy, "w2w_d", w2w, U32)
         x2w = pick("x2w", xw, two_l, U32)
-        x2s = pick("x2s", xs, two_l, U8)
         b_ps = [psum.tile([P, N], F32, name=f"b_ps{t}", tag=f"bank{4 + t}") for t in range(PACK)]
         for t in range(PACK):
             product(b_ps[t][:], w2w_d, w2s_d, t, x2w[:], x2s[:])
         w1w_d = deal(nc.scalar.copy, "w1w_d", w1w, U32)
         x1w = pick("x1w", xw, offs_l, U32)
-        x1s = pick("x1s", xs, offs_l, U8)
-        w1s_d = deal(nc.vector.tensor_copy, "w1s_d", w1s, U8)
+        w1s_d = deal_bytes("w1s_d", w1s)
         a_ps = [psum.tile([P, N], F32, name=f"a_ps{t}", tag=f"bank{t}") for t in range(PACK)]
         for t in range(PACK):
             product(a_ps[t][:], w1w_d, w1s_d, t, x1w[:], x1s[:])
@@ -115,7 +119,7 @@ def tile_picked_keymed_none_po_kernel(
         hi = tile("hi", [P, PACK, N], BF16)
         mid = tile("mid", [P, PACK, N], BF16)
         z = tile("z", [P, PACK, N], BF16)
-        sig = {}
+        sig = [tile("sig0", [P, PACK, HALF], F32)]
         z2 = tile("z2", [P, PACK, N], BF16)
         z_in = tile("z_in", [P, PACK * N], BF16)
         z2_in = tile("z2_in", [P, PACK * N], BF16)
@@ -141,44 +145,46 @@ def tile_picked_keymed_none_po_kernel(
         def median(t):
             nc.vector.tensor_tensor(hi[:, t, :], k1[t][:], k2[t][:], ALU.max)
             nc.vector.tensor_tensor(lo[:, t, :], k1[t][:], k2[t][:], ALU.min)
-            nc.vector.tensor_tensor(mid[:, t, :], a_sb[t][:], hi[:, t, :], ALU.min)
+            nc.vector.scalar_tensor_tensor(mid[:, t, :], a_ps[t][:], ga_t[:, t : t + 1], hi[:, t, :], ALU.mult, ALU.min)
             nc.vector.tensor_tensor(z[:, t, :], lo[:, t, :], mid[:, t, :], ALU.max)
 
-        def gate(t, h, fetch, tag):
-            sig[t, h] = tile(f"sig{t}{h}", [P, HALF], F32, tag)
-            fetch(sig[t, h][:], b_sb[t], nq_l, h)
+        def gate(t, h, fetch):
+            fetch(sig[h][:, t, :], b_sb[t], nq_l, h)
 
         def weave(dst, src):
             nc.vector.tensor_copy(dst.rearrange("p (c i t) -> p c t i", i=4, t=PACK), src.rearrange("p t (c i) -> p c t i", i=4))
 
         def queries(h):
             for t in range(PACK):
-                nc.vector.scalar_tensor_tensor(z2[:, t, cols(h)], b_ps[t][:, cols(h)], gb_t[:, t : t + 1], sig[t, h][:], ALU.mult, ALU.mult)
+                nc.vector.scalar_tensor_tensor(z2[:, t, cols(h)], b_ps[t][:, cols(h)], gb_t[:, t : t + 1], sig[h][:, t, :], ALU.mult, ALU.mult)
             wide = slice(h * PACK * HALF, (h + 1) * PACK * HALF)
             weave(z2_in[:, wide], z2[:, :, cols(h)])
             nc.vector.quantize_mx(z2w[:, cols(h)].bitcast(FP8X4), z2s[:, cols(h)], z2_in[:, wide])
 
         for t in range(PACK):
             nc.scalar.activation(b_sb[t][:], b_ps[t][:], ACT.Sigmoid)
-        gate(3, 0, fetch_scalar, None)
         leave_a(0)
         keys(0, 0)
-        for t in range(PACK - 1):
-            gate(t, 0, fetch_vector, None)
+        for t in range(PACK):
+            gate(t, 0, fetch_vector)
         leave_a(1)
+        leave_a(2)
         keys(1, 0)
         queries(0)
         median(0)
-        leave_a(2)
+        keys(2, 4)
         leave_a(3)
+        keys(3, 0)
         median(1)
-        keys(2, 2)
-        keys(3, 1)
         median(2)
+        sig.append(tile("sig1", [P, PACK, HALF], F32, "a_sb3"))
         for t in range(PACK):
-            gate(t, 1, fetch_scalar, f"k{1 + t % 2}_{t // 2}")
+            gate(t, 1, fetch_scalar)
         median(3)
-        nc.vector.tensor_copy(z_in[:].rearrange("p (u m t) -> p m t u", u=PACK, t=PACK), z[:].rearrange("p t (m u) -> p m t u", u=PACK))
+        z_dealt = z_in[:].rearrange("p (u m t) -> p m t u", u=PACK, t=PACK)
+        z_rows = z[:].rearrange("p t (m u) -> p m t u", u=PACK)
+        nc.vector.tensor_copy(z_dealt[:, P // 2 :], z_rows[:, P // 2 :])
+        nc.scalar.copy(z_dealt[:, : P // 2], z_rows[:, : P // 2])
         nc.vector.quantize_mx(zw[:].bitcast(FP8X4), zs[:], z_in[:])
 
         s_ps = [[psum.tile([P, 2, HALF], F32, name=f"s_ps{h}{u}", tag=f"bank{2 * h + u}") for u in range(2)] for h in range(2)]

@@ -57,28 +57,28 @@ def tile_picked_keymed_none_po_kernel(
         w2s = tile("w2s", [P, N], U8)
         xs = tile("xs", [P, T], U8)
         nc.gpsimd.memset(xs[:].bitcast(I32), 0)
-        nc.vector.memset(w2s[:].bitcast(I32), 0)
+        nc.gpsimd.memset(w2s[:].bitcast(I32), 0)
         nc.gpsimd.memset(w1s[:].bitcast(I32), 0)
 
         two_l = load_list("two_l", two)
         offs_l = load_list("offs_l", offs)
+        w2w = load_words("w2w", w2_words, N)
         load_scales(nc.sync, xs, x_scales)
         xw = load_words("xw", x_words, T)
-        w2w = load_words("w2w", w2_words, N)
         load_scales(nc.sync, w2s, w2_scales)
         w1w = load_words("w1w", w1_words, N)
-        load_scales(nc.gpsimd, w1s, w1_scales)
         nq_l = load_list("nq_l", nq)
         ga_t = tile("ga_t", [P, PACK], F32)
         gb_t = tile("gb_t", [P, PACK], F32)
         nc.sync.dma_start(ga_t[:], ga.rearrange("(p t) o -> p (t o)", t=PACK))
+        load_scales(nc.sync, w1s, w1_scales)
         n1_l = load_list("n1_l", n1)
         n2_l = load_list("n2_l", n2)
         nc.sync.dma_start(gb_t[:], gb.rearrange("(p t) o -> p (t o)", t=PACK))
         cq_l = load_list("cq_l", cq)
 
-        def deal_bytes(name, src):
-            dealt = tile(name, [P, N], U8)
+        def deal_late(name, src, dtype, tag=None):
+            dealt = tile(name, [P, N], dtype, tag)
             nc.gpsimd.tensor_copy(dealt[:].rearrange("p (t m) -> p t m", t=PACK), src[:].rearrange("p (m t) -> p t m", t=PACK))
             return dealt
 
@@ -96,40 +96,58 @@ def tile_picked_keymed_none_po_kernel(
             m = slice(t * P, (t + 1) * P)
             nc.tensor.matmul_mx(out, lhsT=lw[:, m].bitcast(FP8X4), lhsT_scale=ls[:, m], rhs=rw.bitcast(FP8X4), rhs_scale=rs, start=True, stop=True)
 
+        w2w_d = deal(nc.vector.tensor_copy, "w2w_d", w2w, U32)
         x2s = pick("x2s", xs, two_l, U8)
         x1s = pick("x1s", xs, offs_l, U8)
-        w2s_d = deal_bytes("w2s_d", w2s)
-        w2w_d = deal(nc.scalar.copy, "w2w_d", w2w, U32)
         x2w = pick("x2w", xw, two_l, U32)
+        w2s_d = deal_late("w2s_d", w2s, U8)
         b_ps = [psum.tile([P, N], F32, name=f"b_ps{t}", tag=f"bank{4 + t}") for t in range(PACK)]
         for t in range(PACK):
             product(b_ps[t][:], w2w_d, w2s_d, t, x2w[:], x2s[:])
-        w1w_d = deal(nc.scalar.copy, "w1w_d", w1w, U32)
+        w1w_d = deal_late("w1w_d", w1w, U32)
         x1w = pick("x1w", xw, offs_l, U32)
-        w1s_d = deal_bytes("w1s_d", w1s)
+        w1s_d = deal_late("w1s_d", w1s, U8)
         a_ps = [psum.tile([P, N], F32, name=f"a_ps{t}", tag=f"bank{t}") for t in range(PACK)]
         for t in range(PACK):
             product(a_ps[t][:], w1w_d, w1s_d, t, x1w[:], x1s[:])
 
         a_sb = [tile(f"a_sb{t}", [P, N], F32) for t in range(PACK)]
         b_sb = [tile(f"b_sb{t}", [P, N], F32) for t in range(PACK)]
-        k1 = [tile(f"k1_{t}", [P, N], BF16) for t in range(PACK)]
-        k2 = [tile(f"k2_{t}", [P, N], BF16) for t in range(PACK)]
+        k1 = tile("k1", [P, PACK, N], BF16)
+        k2 = tile("k2", [P, PACK, N], BF16)
         lo = tile("lo", [P, PACK, N], BF16)
         hi = tile("hi", [P, PACK, N], BF16)
         mid = tile("mid", [P, PACK, N], BF16)
         z = tile("z", [P, PACK, N], BF16)
-        sig = [tile("sig0", [P, PACK, HALF], F32)]
+        sig = tile("sig", [P, PACK, N], F32)
         z2 = tile("z2", [P, PACK, N], BF16)
-        z_in = tile("z_in", [P, PACK * N], BF16)
+        z_in = tile("z_in", [P, PACK, N], BF16)
         z2_in = tile("z2_in", [P, PACK * N], BF16)
         zw = tile("zw", [P, N], U32)
         zs = tile("zs", [P, N], U8)
         z2w = tile("z2w", [P, N], U32)
         z2s = tile("z2s", [P, N], U8)
+        s_ps = {}
+        s_sb = [tile(f"s_sb{t}", [P, N], F32) for t in range(PACK)]
+        got = tile("got", [P, PACK, N], F32)
+        res = tile("res", [P, PACK, N], F32)
+        res_in = tile("res_in", [P, PACK * N], BF16)
+        ow = tile("ow", [P, N], U32)
+        osc = tile("osc", [P, N], U8)
+        out_rows = out_0.rearrange("(p t) v -> p t v", t=PACK)
+        out_words = out_1[0].rearrange("p n t -> p (n t)").bitcast(I32)
 
-        def leave_a(t):
-            nc.scalar.activation(a_sb[t][:], a_ps[t][:], ACT.Copy, scale=ga_t[:, t : t + 1])
+        def leave(dst, src, scale, on_vector):
+            if on_vector:
+                nc.vector.tensor_scalar(dst, src, scale, None, ALU.mult)
+            else:
+                nc.scalar.activation(dst, src, ACT.Copy, scale=scale)
+
+        def leave_a(t, on_vector):
+            leave(a_sb[t][:], a_ps[t][:], ga_t[:, t : t + 1], on_vector)
+
+        def leave_s(t, on_vector):
+            leave(s_sb[t][:], s_ps[t][:], -0.03125, on_vector)
 
         def fetch_scalar(out, window, held, h):
             nc.scalar.activation(out, window[:].indirect(half_of(held, h)), ACT.Copy)
@@ -137,95 +155,111 @@ def tile_picked_keymed_none_po_kernel(
         def fetch_vector(out, window, held, h):
             nc.vector.tensor_copy(out, window[:].indirect(half_of(held, h)))
 
-        def keys(t, on_vector):
-            for n, (dst, held, h) in enumerate([(k1, n1_l, 0), (k2, n2_l, 0), (k1, n1_l, 1), (k2, n2_l, 1)]):
-                fetch = fetch_vector if n < on_vector else fetch_scalar
-                fetch(dst[t][:, cols(h)], a_sb[t], held, h)
+        def key(t, h, fetch1, fetch2):
+            fetch1(k1[:, t, cols(h)], a_sb[t], n1_l, h)
+            fetch2(k2[:, t, cols(h)], a_sb[t], n2_l, h)
 
-        def median(t):
-            nc.vector.tensor_tensor(hi[:, t, :], k1[t][:], k2[t][:], ALU.max)
-            nc.vector.tensor_tensor(lo[:, t, :], k1[t][:], k2[t][:], ALU.min)
-            nc.vector.scalar_tensor_tensor(mid[:, t, :], a_ps[t][:], ga_t[:, t : t + 1], hi[:, t, :], ALU.mult, ALU.min)
-            nc.vector.tensor_tensor(z[:, t, :], lo[:, t, :], mid[:, t, :], ALU.max)
+        def median(t, c):
+            nc.vector.tensor_tensor(hi[:, t, c], k1[:, t, c], k2[:, t, c], ALU.max)
+            nc.vector.tensor_tensor(lo[:, t, c], k1[:, t, c], k2[:, t, c], ALU.min)
+            nc.vector.scalar_tensor_tensor(mid[:, t, c], a_ps[t][:, c], ga_t[:, t : t + 1], hi[:, t, c], ALU.mult, ALU.min)
+            nc.vector.tensor_tensor(z[:, t, c], lo[:, t, c], mid[:, t, c], ALU.max)
 
         def gate(t, h, fetch):
-            fetch(sig[h][:, t, :], b_sb[t], nq_l, h)
+            fetch(sig[:, t, cols(h)], b_sb[t], nq_l, h)
 
-        def weave(dst, src):
-            nc.vector.tensor_copy(dst.rearrange("p (c i t) -> p c t i", i=4, t=PACK), src.rearrange("p t (c i) -> p c t i", i=4))
+        def weave(dst, src, copy):
+            copy(dst.rearrange("p (c i t) -> p c t i", i=4, t=PACK), src.rearrange("p t (c i) -> p c t i", i=4))
 
-        def queries(h):
-            for t in range(PACK):
-                nc.vector.scalar_tensor_tensor(z2[:, t, cols(h)], b_ps[t][:, cols(h)], gb_t[:, t : t + 1], sig[h][:, t, :], ALU.mult, ALU.mult)
+        def query(t):
+            nc.vector.scalar_tensor_tensor(z2[:, t, :], b_ps[t][:], gb_t[:, t : t + 1], sig[:, t, :], ALU.mult, ALU.mult)
+
+        def pack_queries(h, copy):
             wide = slice(h * PACK * HALF, (h + 1) * PACK * HALF)
-            weave(z2_in[:, wide], z2[:, :, cols(h)])
+            weave(z2_in[:, wide], z2[:, :, cols(h)], copy)
             nc.vector.quantize_mx(z2w[:, cols(h)].bitcast(FP8X4), z2s[:, cols(h)], z2_in[:, wide])
+
+        def pack_keys(u, copy):
+            m = slice(u * P, (u + 1) * P)
+            copy(z_in[:, u, :].rearrange("p (m t) -> p m t", t=PACK), z[:].rearrange("p t (m u) -> p u m t", u=PACK)[:, u])
+            nc.vector.quantize_mx(zw[:, m].bitcast(FP8X4), zs[:, m], z_in[:, u, :])
+            s_ps[u] = psum.tile([P, N], F32, name=f"s_ps{u}", tag=f"bank{4 + u}")
+            product(s_ps[u][:], zw, zs, u, z2w[:], z2s[:])
+
+        def result(t, c):
+            nc.vector.scalar_tensor_tensor(res[:, t, c], s_ps[t][:, c], 0.0625, got[:, t, c], ALU.mult, ALU.add)
+
+        def store(ts, c):
+            nc.sync.dma_start(out_rows[:, ts, c], res[:, ts, c])
+
+        def planes(h, copy):
+            wide = slice(h * PACK * HALF, (h + 1) * PACK * HALF)
+            weave(res_in[:, wide], res[:, :, cols(h)], copy)
+            nc.vector.quantize_mx(ow[:, cols(h)].bitcast(FP8X4), osc[:, cols(h)], res_in[:, wide])
+            nc.sync.dma_start(out_words[:, cols(h)], ow[:, cols(h)].bitcast(I32))
 
         for t in range(PACK):
             nc.scalar.activation(b_sb[t][:], b_ps[t][:], ACT.Sigmoid)
-        leave_a(0)
-        keys(0, 0)
-        for t in range(PACK):
-            gate(t, 0, fetch_vector)
-        leave_a(1)
-        leave_a(2)
-        keys(1, 0)
-        queries(0)
-        median(0)
-        keys(2, 4)
-        leave_a(3)
-        keys(3, 0)
-        median(1)
-        median(2)
-        sig.append(tile("sig1", [P, PACK, HALF], F32, "a_sb3"))
-        for t in range(PACK):
-            gate(t, 1, fetch_scalar)
-        median(3)
-        z_dealt = z_in[:].rearrange("p (u m t) -> p m t u", u=PACK, t=PACK)
-        z_rows = z[:].rearrange("p t (m u) -> p m t u", u=PACK)
-        nc.vector.tensor_copy(z_dealt[:, P // 2 :], z_rows[:, P // 2 :])
-        nc.scalar.copy(z_dealt[:, : P // 2], z_rows[:, : P // 2])
-        nc.vector.quantize_mx(zw[:].bitcast(FP8X4), zs[:], z_in[:])
-
-        s_ps = [[psum.tile([P, 2, HALF], F32, name=f"s_ps{h}{u}", tag=f"bank{2 * h + u}") for u in range(2)] for h in range(2)]
-        s_sb = [tile(f"s_sb{t}", [P, N], F32) for t in range(PACK)]
-        got = tile("got", [P, PACK, N], F32)
-        res = tile("res", [P, PACK, N], F32)
-        res_in = tile("res_in", [P, PACK * N], BF16)
-        ow = tile("ow", [P, N], U32)
-        osc = tile("osc", [P, N], U8)
-
-        def scores(h):
-            for t in range(PACK):
-                product(s_ps[h][t // 2][:, t % 2, :], zw, zs, t, z2w[:, cols(h)], z2s[:, cols(h)])
-
-        def leave_s(t, h, on_vector):
-            src = s_ps[h][t // 2][:, t % 2, :]
-            if on_vector:
-                nc.vector.tensor_scalar(s_sb[t][:, cols(h)], src, -0.03125, None, ALU.mult)
-            else:
-                nc.scalar.activation(s_sb[t][:, cols(h)], src, ACT.Copy, scale=-0.03125)
-
-        scores(0)
-        for t in range(PACK):
-            leave_s(t, 0, False)
-        queries(1)
-        scores(1)
-        for t in range(PACK):
-            leave_s(t, 1, t >= 2)
-
-        out_rows = out_0.rearrange("(p t) v -> p t v", t=PACK)
-        out_words = out_1[0].rearrange("p n t -> p (n t)").bitcast(I32)
+        gate(0, 0, fetch_vector)
+        gate(0, 1, fetch_vector)
+        gate(1, 0, fetch_vector)
+        gate(1, 1, fetch_vector)
+        query(0)
+        query(1)
+        leave_a(0, False)
+        key(0, 0, fetch_scalar, fetch_scalar)
+        key(0, 1, fetch_scalar, fetch_scalar)
+        gate(2, 0, fetch_vector)
+        gate(2, 1, fetch_vector)
+        gate(3, 0, fetch_vector)
+        gate(3, 1, fetch_scalar)
+        query(2)
+        query(3)
+        leave_a(1, False)
+        key(1, 0, fetch_scalar, fetch_scalar)
+        key(1, 1, fetch_scalar, fetch_scalar)
+        weave(z2_in[:], z2[:], nc.vector.tensor_copy)
+        nc.vector.quantize_mx(z2w[:].bitcast(FP8X4), z2s[:], z2_in[:])
+        median(0, slice(0, N))
+        leave_a(2, False)
+        key(2, 0, fetch_scalar, fetch_scalar)
+        key(2, 1, fetch_scalar, fetch_scalar)
+        median(1, slice(0, N))
+        leave_a(3, False)
+        key(3, 0, fetch_scalar, fetch_scalar)
+        key(3, 1, fetch_scalar, fetch_scalar)
+        median(2, slice(0, N))
+        median(3, cols(0))
+        median(3, cols(1))
+        pack_keys(0, nc.vector.tensor_copy)
+        pack_keys(1, nc.vector.tensor_copy)
+        pack_keys(2, nc.scalar.copy)
+        pack_keys(3, nc.scalar.copy)
+        leave_s(0, True)
+        leave_s(1, False)
+        fetch_vector(got[:, 0, cols(0)], s_sb[0], cq_l, 0)
+        fetch_vector(got[:, 0, cols(1)], s_sb[0], cq_l, 1)
+        result(0, slice(0, N))
+        store(slice(0, 1), slice(0, N))
+        fetch_scalar(got[:, 1, cols(0)], s_sb[1], cq_l, 0)
+        fetch_scalar(got[:, 1, cols(1)], s_sb[1], cq_l, 1)
+        leave_s(2, False)
+        leave_s(3, True)
+        fetch_scalar(got[:, 2, cols(0)], s_sb[2], cq_l, 0)
+        fetch_scalar(got[:, 2, cols(1)], s_sb[2], cq_l, 1)
+        result(1, slice(0, N))
+        store(slice(1, 2), slice(0, N))
+        fetch_vector(got[:, 3, cols(0)], s_sb[3], cq_l, 0)
+        fetch_scalar(got[:, 3, cols(1)], s_sb[3], cq_l, 1)
+        result(2, slice(0, N))
+        store(slice(2, 3), slice(0, N))
+        result(3, slice(0, N))
+        store(slice(3, 4), slice(0, N))
+        cut = 320
+        weave(res_in[:, : PACK * cut], res[:, :, :cut], nc.vector.tensor_copy)
+        weave(res_in[:, PACK * cut :], res[:, :, cut:], nc.scalar.copy)
         for h in range(2):
-            for u in range(2):
-                for t in (2 * u, 2 * u + 1):
-                    fetch = fetch_vector if h == 0 and t >= 2 else fetch_scalar
-                    fetch(got[:, t, cols(h)], s_sb[t], cq_l, h)
-                pair = slice(2 * u, 2 * u + 2)
-                nc.vector.scalar_tensor_tensor(res[:, pair, cols(h)], s_ps[h][u][:], 0.0625, got[:, pair, cols(h)], ALU.mult, ALU.add)
-                nc.sync.dma_start(out_rows[:, pair, cols(h)], res[:, pair, cols(h)])
             wide = slice(h * PACK * HALF, (h + 1) * PACK * HALF)
-            weave(res_in[:, wide], res[:, :, cols(h)])
             nc.vector.quantize_mx(ow[:, cols(h)].bitcast(FP8X4), osc[:, cols(h)], res_in[:, wide])
             nc.sync.dma_start(out_words[:, cols(h)], ow[:, cols(h)].bitcast(I32))
         for q in range(4):

@@ -18,7 +18,10 @@ T = 2048
 N = 512
 HALF = N // 2
 LIST_COLS = N // 16
-FLOPS = 3 * 2 * 512 * 512 * 512
+QUADRANTS = 4
+BANKS = 8
+S_SCALE = 0.0625
+FLOPS = 3 * 2 * N * N * N
 
 
 def tile_picked_keymed_none_po_kernel(
@@ -30,8 +33,17 @@ def tile_picked_keymed_none_po_kernel(
         sb = ctx.enter_context(tc.tile_pool(name="sb", bufs=1))
         psum = ctx.enter_context(tc.psum_pool(name="psum", bufs=1))
 
-        def tile(name, shape, dtype, tag=None):
-            return sb.tile(shape, dtype, name=name, tag=tag or name, align_bytes=64)
+        def tile(name, shape, dtype, reuses=None):
+            return sb.tile(shape, dtype, name=name, tag=reuses or name, align_bytes=64)
+
+        def bank(name, width, number):
+            return psum.tile([P, width], F32, name=name, tag=f"bank{number}")
+
+        def cols(h):
+            return slice(h * HALF, (h + 1) * HALF)
+
+        def scale_rows(held, q):
+            return held[32 * q : 32 * q + 4, :].bitcast(I32)
 
         def load_list(name, src):
             held = lists.tile([P, LIST_COLS], U16, name=name)
@@ -43,121 +55,115 @@ def tile_picked_keymed_none_po_kernel(
             nc.sync.dma_start(held[:].bitcast(I32), src[0].rearrange("p n t -> p (n t)").bitcast(I32))
             return held
 
-        def load_scales(queue, held, src, quadrants=range(4)):
-            for q in quadrants:
-                queue.dma_start(held[32 * q : 32 * q + 4, :].bitcast(I32), src[0, 4 * q : 4 * q + 4, :].bitcast(I32))
+        def load_scales(held, src):
+            for q in range(QUADRANTS):
+                nc.sync.dma_start(scale_rows(held, q), src[0, 4 * q : 4 * q + 4, :].bitcast(I32))
 
-        def half_of(held, h):
-            return held[:, h * (LIST_COLS // 2) : (h + 1) * (LIST_COLS // 2)]
+        def load_gain(name, src):
+            held = tile(name, [P, PACK], F32)
+            nc.sync.dma_start(held[:], src.rearrange("(p t) o -> p (t o)", t=PACK))
+            return held
 
-        def cols(h):
-            return slice(h * HALF, (h + 1) * HALF)
-
-        w1s = tile("w1s", [P, N], U8)
-        w2s = tile("w2s", [P, N], U8)
         xs = tile("xs", [P, T], U8)
-        nc.gpsimd.memset(xs[:].bitcast(I32), 0)
-        nc.gpsimd.memset(w2s[:].bitcast(I32), 0)
-        nc.gpsimd.memset(w1s[:].bitcast(I32), 0)
+        w2s = tile("w2s", [P, N], U8)
+        w1s = tile("w1s", [P, N], U8)
+        for held in (xs, w2s, w1s):
+            nc.gpsimd.memset(held[:].bitcast(I32), 0)
 
         two_l = load_list("two_l", two)
         offs_l = load_list("offs_l", offs)
         w2w = load_words("w2w", w2_words, N)
-        load_scales(nc.sync, xs, x_scales)
+        load_scales(xs, x_scales)
         xw = load_words("xw", x_words, T)
-        load_scales(nc.sync, w2s, w2_scales)
+        load_scales(w2s, w2_scales)
         w1w = load_words("w1w", w1_words, N)
         nq_l = load_list("nq_l", nq)
-        ga_t = tile("ga_t", [P, PACK], F32)
-        gb_t = tile("gb_t", [P, PACK], F32)
-        nc.sync.dma_start(ga_t[:], ga.rearrange("(p t) o -> p (t o)", t=PACK))
-        load_scales(nc.sync, w1s, w1_scales)
+        ga_t = load_gain("ga_t", ga)
+        load_scales(w1s, w1_scales)
         n1_l = load_list("n1_l", n1)
         n2_l = load_list("n2_l", n2)
-        nc.sync.dma_start(gb_t[:], gb.rearrange("(p t) o -> p (t o)", t=PACK))
+        gb_t = load_gain("gb_t", gb)
         cq_l = load_list("cq_l", cq)
-
-        def deal_late(name, src, dtype, tag=None):
-            dealt = tile(name, [P, N], dtype, tag)
-            nc.gpsimd.tensor_copy(dealt[:].rearrange("p (t m) -> p t m", t=PACK), src[:].rearrange("p (m t) -> p t m", t=PACK))
-            return dealt
 
         def deal(copy, name, src, dtype):
             dealt = tile(name, [P, N], dtype)
             copy(dealt[:].rearrange("p (t m) -> p m t", t=PACK), src[:].rearrange("p (m t) -> p m t", t=PACK))
             return dealt
 
-        def pick(name, window, offsets, dtype):
-            picked = tile(name, [P, N], dtype)
+        def pick(name, window, offsets, dtype, reuses=None):
+            picked = tile(name, [P, N], dtype, reuses)
             nc.vector.tensor_copy(picked[:], window[:].indirect(offsets[:]))
             return picked
 
-        def product(out, lw, ls, t, rw, rs):
+        def product(out, dealt_words, dealt_scales, t, words, scales):
             m = slice(t * P, (t + 1) * P)
-            nc.tensor.matmul_mx(out, lhsT=lw[:, m].bitcast(FP8X4), lhsT_scale=ls[:, m], rhs=rw.bitcast(FP8X4), rhs_scale=rs, start=True, stop=True)
+            nc.tensor.matmul_mx(
+                out,
+                lhsT=dealt_words[:, m].bitcast(FP8X4),
+                lhsT_scale=dealt_scales[:, m],
+                rhs=words.bitcast(FP8X4),
+                rhs_scale=scales,
+                start=True,
+                stop=True,
+            )
 
-        w2w_d = deal(nc.vector.tensor_copy, "w2w_d", w2w, U32)
+        w2w_d = deal(nc.scalar.copy, "w2w_d", w2w, U32)
         x2s = pick("x2s", xs, two_l, U8)
         x1s = pick("x1s", xs, offs_l, U8)
         x2w = pick("x2w", xw, two_l, U32)
-        w2s_d = deal_late("w2s_d", w2s, U8)
-        b_ps = [psum.tile([P, N], F32, name=f"b_ps{t}", tag=f"bank{4 + t}") for t in range(PACK)]
+        w2s_d = deal(nc.vector.tensor_copy, "w2s_d", w2s, U8)
+        b_ps = [bank(f"b_ps{t}", N, PACK + t) for t in range(PACK)]
         for t in range(PACK):
             product(b_ps[t][:], w2w_d, w2s_d, t, x2w[:], x2s[:])
-        w1w_d = deal_late("w1w_d", w1w, U32)
-        x1w = pick("x1w", xw, offs_l, U32)
-        w1s_d = deal_late("w1s_d", w1s, U8)
-        a_ps = [psum.tile([P, N], F32, name=f"a_ps{t}", tag=f"bank{t}") for t in range(PACK)]
+        w1w_d = deal(nc.vector.tensor_copy, "w1w_d", w1w, U32)
+        x1w = pick("x1w", xw, offs_l, U32, reuses="w2s")
+        w1s_d = deal(nc.vector.tensor_copy, "w1s_d", w1s, U8)
+        a_ps = [bank(f"a_ps{t}", N, t) for t in range(PACK)]
         for t in range(PACK):
             product(a_ps[t][:], w1w_d, w1s_d, t, x1w[:], x1s[:])
 
-        a_sb = [tile(f"a_sb{t}", [P, N], F32) for t in range(PACK)]
-        b_sb = [tile(f"b_sb{t}", [P, N], F32) for t in range(PACK)]
+        def looked_up(window, held, h):
+            return window[:].indirect(held[:, h * (LIST_COLS // 2) : (h + 1) * (LIST_COLS // 2)])
+
+        def fetch_scalar(out, window, held, h):
+            nc.scalar.activation(out, looked_up(window, held, h), ACT.Copy)
+
+        def fetch_vector(out, window, held, h):
+            nc.vector.tensor_copy(out, looked_up(window, held, h))
+
+        def weave(copy, dst, src):
+            copy(dst.rearrange("p (c i t) -> p c t i", i=4, t=PACK), src.rearrange("p t (c i) -> p c t i", i=4))
+
+        sig_rows = [tile(f"sig_rows{t}", [P, N], F32) for t in range(PACK)]
+        gate = tile("gate", [P, PACK, N], F32, reuses="w1s")
+        z2 = tile("z2", [P, PACK, N], BF16)
+        z2_in = tile("z2_in", [P, PACK * N], BF16)
+        z2w = tile("z2w", [P, N], U32)
+        z2s = tile("z2s", [P, N], U8)
+        a_rows = [tile(f"a_rows{t}", [P, N], F32) for t in range(PACK)]
+
+        def leave_a(t):
+            nc.scalar.activation(a_rows[t][:], a_ps[t][:], ACT.Copy, scale=ga_t[:, t : t + 1])
+
+        for t in range(PACK):
+            nc.scalar.activation(sig_rows[t][:], b_ps[t][:], ACT.Sigmoid)
+        leave_a(0)
+        for pair in ((0, 1), (2, 3)):
+            for t in pair:
+                for h in range(2):
+                    fetch = fetch_scalar if (t, h) == (PACK - 1, 1) else fetch_vector
+                    fetch(gate[:, t, cols(h)], sig_rows[t], nq_l, h)
+            for t in pair:
+                nc.vector.scalar_tensor_tensor(z2[:, t, :], b_ps[t][:], gb_t[:, t : t + 1], gate[:, t, :], ALU.mult, ALU.mult)
+        weave(nc.vector.tensor_copy, z2_in[:], z2[:])
+        nc.vector.quantize_mx(z2w[:].bitcast(FP8X4), z2s[:], z2_in[:])
+
         k1 = tile("k1", [P, PACK, N], BF16)
         k2 = tile("k2", [P, PACK, N], BF16)
         lo = tile("lo", [P, PACK, N], BF16)
         hi = tile("hi", [P, PACK, N], BF16)
         mid = tile("mid", [P, PACK, N], BF16)
         z = tile("z", [P, PACK, N], BF16)
-        sig = tile("sig", [P, PACK, N], F32)
-        z2 = tile("z2", [P, PACK, N], BF16)
-        z_in = tile("z_in", [P, PACK, N], BF16)
-        z2_in = tile("z2_in", [P, PACK * N], BF16)
-        zw = tile("zw", [P, N], U32)
-        zs = tile("zs", [P, N], U8)
-        z2w = tile("z2w", [P, N], U32)
-        z2s = tile("z2s", [P, N], U8)
-        s_ps = {}
-        s_sb = [tile(f"s_sb{t}", [P, N], F32) for t in range(PACK)]
-        got = tile("got", [P, PACK, N], F32)
-        res = tile("res", [P, PACK, N], F32)
-        res_in = tile("res_in", [P, PACK * N], BF16)
-        ow = tile("ow", [P, N], U32)
-        osc = tile("osc", [P, N], U8)
-        out_rows = out_0.rearrange("(p t) v -> p t v", t=PACK)
-        out_words = out_1[0].rearrange("p n t -> p (n t)").bitcast(I32)
-
-        def leave(dst, src, scale, on_vector):
-            if on_vector:
-                nc.vector.tensor_scalar(dst, src, scale, None, ALU.mult)
-            else:
-                nc.scalar.activation(dst, src, ACT.Copy, scale=scale)
-
-        def leave_a(t, on_vector):
-            leave(a_sb[t][:], a_ps[t][:], ga_t[:, t : t + 1], on_vector)
-
-        def leave_s(t, on_vector):
-            leave(s_sb[t][:], s_ps[t][:], -0.03125, on_vector)
-
-        def fetch_scalar(out, window, held, h):
-            nc.scalar.activation(out, window[:].indirect(half_of(held, h)), ACT.Copy)
-
-        def fetch_vector(out, window, held, h):
-            nc.vector.tensor_copy(out, window[:].indirect(half_of(held, h)))
-
-        def key(t, h, fetch1, fetch2):
-            fetch1(k1[:, t, cols(h)], a_sb[t], n1_l, h)
-            fetch2(k2[:, t, cols(h)], a_sb[t], n2_l, h)
 
         def median(t, c):
             nc.vector.tensor_tensor(hi[:, t, c], k1[:, t, c], k2[:, t, c], ALU.max)
@@ -165,103 +171,86 @@ def tile_picked_keymed_none_po_kernel(
             nc.vector.scalar_tensor_tensor(mid[:, t, c], a_ps[t][:, c], ga_t[:, t : t + 1], hi[:, t, c], ALU.mult, ALU.min)
             nc.vector.tensor_tensor(z[:, t, c], lo[:, t, c], mid[:, t, c], ALU.max)
 
-        def gate(t, h, fetch):
-            fetch(sig[:, t, cols(h)], b_sb[t], nq_l, h)
+        for t in range(PACK):
+            if t > 0:
+                leave_a(t)
+            for h in range(2):
+                fetch_scalar(k1[:, t, cols(h)], a_rows[t], n1_l, h)
+                fetch_scalar(k2[:, t, cols(h)], a_rows[t], n2_l, h)
+            for c in [cols(0), cols(1)] if t == PACK - 1 else [slice(0, N)]:
+                median(t, c)
 
-        def weave(dst, src, copy):
-            copy(dst.rearrange("p (c i t) -> p c t i", i=4, t=PACK), src.rearrange("p t (c i) -> p c t i", i=4))
-
-        def query(t):
-            nc.vector.scalar_tensor_tensor(z2[:, t, :], b_ps[t][:], gb_t[:, t : t + 1], sig[:, t, :], ALU.mult, ALU.mult)
-
-        def pack_queries(h, copy):
-            wide = slice(h * PACK * HALF, (h + 1) * PACK * HALF)
-            weave(z2_in[:, wide], z2[:, :, cols(h)], copy)
-            nc.vector.quantize_mx(z2w[:, cols(h)].bitcast(FP8X4), z2s[:, cols(h)], z2_in[:, wide])
-
-        def pack_keys(u, copy):
+        z_in = tile("z_in", [P, PACK, N], BF16)
+        zw = tile("zw", [P, N], U32)
+        zs = tile("zs", [P, N], U8)
+        z_dealt = z[:].rearrange("p t (m u) -> p u m t", u=PACK)
+        s_ps = {}
+        for u in range(PACK):
+            copy = nc.vector.tensor_copy if u < 2 else nc.scalar.copy
+            copy(z_in[:, u, :].rearrange("p (m t) -> p m t", t=PACK), z_dealt[:, u])
             m = slice(u * P, (u + 1) * P)
-            copy(z_in[:, u, :].rearrange("p (m t) -> p m t", t=PACK), z[:].rearrange("p t (m u) -> p u m t", u=PACK)[:, u])
             nc.vector.quantize_mx(zw[:, m].bitcast(FP8X4), zs[:, m], z_in[:, u, :])
-            s_ps[u] = psum.tile([P, N], F32, name=f"s_ps{u}", tag=f"bank{4 + u}")
-            product(s_ps[u][:], zw, zs, u, z2w[:], z2s[:])
+            for h in range(2):
+                s_ps[u, h] = bank(f"s_ps{u}{h}", HALF, (PACK + 2 * u + h) % BANKS)
+                product(s_ps[u, h][:], zw, zs, u, z2w[:, cols(h)], z2s[:, cols(h)])
 
-        def result(t, c):
-            nc.vector.scalar_tensor_tensor(res[:, t, c], s_ps[t][:, c], 0.0625, got[:, t, c], ALU.mult, ALU.add)
+        s_rows = [tile(f"s_rows{t}", [P, N], F32) for t in range(PACK)]
+        got = tile("got", [P, PACK, N], F32)
+        res = tile("res", [P, PACK, N], F32)
+        res_in = tile("res_in", [P, PACK * N], BF16)
+        out_w = tile("out_w", [P, N], U32)
+        out_s = tile("out_s", [P, N], U8)
+        out_rows = out_0.rearrange("(p t) v -> p t v", t=PACK)
+        out_words = out_1[0].rearrange("p n t -> p (n t)").bitcast(I32)
+
+        def leave_s_scalar(t, h):
+            nc.scalar.activation(s_rows[t][:, cols(h)], s_ps[t, h][:], ACT.Copy, scale=-0.5 * S_SCALE)
+
+        def leave_s_vector(t, h):
+            nc.vector.tensor_scalar(s_rows[t][:, cols(h)], s_ps[t, h][:], -0.5 * S_SCALE, None, ALU.mult)
+
+        def other_column(fetch, t, h):
+            fetch(got[:, t, cols(h)], s_rows[t], cq_l, h)
+
+        def result(t, h):
+            nc.vector.scalar_tensor_tensor(res[:, t, cols(h)], s_ps[t, h][:], S_SCALE, got[:, t, cols(h)], ALU.mult, ALU.add)
 
         def store(ts, c):
             nc.sync.dma_start(out_rows[:, ts, c], res[:, ts, c])
 
-        def planes(h, copy):
+        def planes(copy, h):
             wide = slice(h * PACK * HALF, (h + 1) * PACK * HALF)
-            weave(res_in[:, wide], res[:, :, cols(h)], copy)
-            nc.vector.quantize_mx(ow[:, cols(h)].bitcast(FP8X4), osc[:, cols(h)], res_in[:, wide])
-            nc.sync.dma_start(out_words[:, cols(h)], ow[:, cols(h)].bitcast(I32))
+            weave(copy, res_in[:, wide], res[:, :, cols(h)])
+            nc.vector.quantize_mx(out_w[:, cols(h)].bitcast(FP8X4), out_s[:, cols(h)], res_in[:, wide])
+            nc.sync.dma_start(out_words[:, cols(h)], out_w[:, cols(h)].bitcast(I32))
 
-        for t in range(PACK):
-            nc.scalar.activation(b_sb[t][:], b_ps[t][:], ACT.Sigmoid)
-        gate(0, 0, fetch_vector)
-        gate(0, 1, fetch_vector)
-        gate(1, 0, fetch_vector)
-        gate(1, 1, fetch_vector)
-        query(0)
-        query(1)
-        leave_a(0, False)
-        key(0, 0, fetch_scalar, fetch_scalar)
-        key(0, 1, fetch_scalar, fetch_scalar)
-        gate(2, 0, fetch_vector)
-        gate(2, 1, fetch_vector)
-        gate(3, 0, fetch_vector)
-        gate(3, 1, fetch_scalar)
-        query(2)
-        query(3)
-        leave_a(1, False)
-        key(1, 0, fetch_scalar, fetch_scalar)
-        key(1, 1, fetch_scalar, fetch_scalar)
-        weave(z2_in[:], z2[:], nc.vector.tensor_copy)
-        nc.vector.quantize_mx(z2w[:].bitcast(FP8X4), z2s[:], z2_in[:])
-        median(0, slice(0, N))
-        leave_a(2, False)
-        key(2, 0, fetch_scalar, fetch_scalar)
-        key(2, 1, fetch_scalar, fetch_scalar)
-        median(1, slice(0, N))
-        leave_a(3, False)
-        key(3, 0, fetch_scalar, fetch_scalar)
-        key(3, 1, fetch_scalar, fetch_scalar)
-        median(2, slice(0, N))
-        median(3, cols(0))
-        median(3, cols(1))
-        pack_keys(0, nc.vector.tensor_copy)
-        pack_keys(1, nc.vector.tensor_copy)
-        pack_keys(2, nc.scalar.copy)
-        pack_keys(3, nc.scalar.copy)
-        leave_s(0, True)
-        leave_s(1, False)
-        fetch_vector(got[:, 0, cols(0)], s_sb[0], cq_l, 0)
-        fetch_vector(got[:, 0, cols(1)], s_sb[0], cq_l, 1)
-        result(0, slice(0, N))
-        store(slice(0, 1), slice(0, N))
-        fetch_scalar(got[:, 1, cols(0)], s_sb[1], cq_l, 0)
-        fetch_scalar(got[:, 1, cols(1)], s_sb[1], cq_l, 1)
-        leave_s(2, False)
-        leave_s(3, True)
-        fetch_scalar(got[:, 2, cols(0)], s_sb[2], cq_l, 0)
-        fetch_scalar(got[:, 2, cols(1)], s_sb[2], cq_l, 1)
-        result(1, slice(0, N))
-        store(slice(1, 2), slice(0, N))
-        fetch_vector(got[:, 3, cols(0)], s_sb[3], cq_l, 0)
-        fetch_scalar(got[:, 3, cols(1)], s_sb[3], cq_l, 1)
-        result(2, slice(0, N))
-        store(slice(2, 3), slice(0, N))
-        result(3, slice(0, N))
-        store(slice(3, 4), slice(0, N))
-        cut = 320
-        weave(res_in[:, : PACK * cut], res[:, :, :cut], nc.vector.tensor_copy)
-        weave(res_in[:, PACK * cut :], res[:, :, cut:], nc.scalar.copy)
+        leave_s_vector(0, 0)
+        leave_s_scalar(0, 1)
         for h in range(2):
-            wide = slice(h * PACK * HALF, (h + 1) * PACK * HALF)
-            nc.vector.quantize_mx(ow[:, cols(h)].bitcast(FP8X4), osc[:, cols(h)], res_in[:, wide])
-            nc.sync.dma_start(out_words[:, cols(h)], ow[:, cols(h)].bitcast(I32))
-        for q in range(4):
+            leave_s_scalar(1, h)
+        for h in range(2):
+            other_column(fetch_vector, 0, h)
+        for h in range(2):
+            result(0, h)
+        store(slice(0, 1), slice(0, N))
+        for h in range(2):
+            other_column(fetch_scalar, 1, h)
+        for h in range(2):
+            leave_s_scalar(2, h)
+        for h in range(2):
+            leave_s_vector(3, h)
+        other_column(fetch_scalar, 2, 0)
+        other_column(fetch_vector, 3, 0)
+        other_column(fetch_scalar, 2, 1)
+        other_column(fetch_scalar, 3, 1)
+        for h in range(2):
+            result(1, h)
+        store(slice(1, 2), slice(0, N))
+        for h, copy in ((0, nc.scalar.copy), (1, nc.vector.tensor_copy)):
+            result(2, h)
+            result(3, h)
+            store(slice(2, PACK), cols(h))
+            planes(copy, h)
+        for q in range(QUADRANTS):
             queue = nc.scalar if q % 2 else nc.sync
-            queue.dma_start(out_2[0, 4 * q : 4 * q + 4, :].bitcast(I32), osc[32 * q : 32 * q + 4, :].bitcast(I32))
+            queue.dma_start(out_2[0, 4 * q : 4 * q + 4, :].bitcast(I32), scale_rows(out_s, q))

@@ -19,7 +19,8 @@ N = 512
 HALF = N // 2
 LIST_COLS = N // 16
 QUADRANTS = 4
-BANKS = 8
+WHOLE = slice(0, N)
+WEAVE_CUT = 320
 S_SCALE = 0.0625
 FLOPS = 3 * 2 * N * N * N
 
@@ -33,8 +34,8 @@ def tile_picked_keymed_none_po_kernel(
         sb = ctx.enter_context(tc.tile_pool(name="sb", bufs=1))
         psum = ctx.enter_context(tc.psum_pool(name="psum", bufs=1))
 
-        def tile(name, shape, dtype, reuses=None):
-            return sb.tile(shape, dtype, name=name, tag=reuses or name, align_bytes=64)
+        def tile(name, shape, dtype):
+            return sb.tile(shape, dtype, name=name, align_bytes=64)
 
         def bank(name, width, number):
             return psum.tile([P, width], F32, name=name, tag=f"bank{number}")
@@ -85,13 +86,18 @@ def tile_picked_keymed_none_po_kernel(
         gb_t = load_gain("gb_t", gb)
         cq_l = load_list("cq_l", cq)
 
-        def deal(copy, name, src, dtype):
+        def deal_vector(name, src, dtype):
             dealt = tile(name, [P, N], dtype)
-            copy(dealt[:].rearrange("p (t m) -> p m t", t=PACK), src[:].rearrange("p (m t) -> p m t", t=PACK))
+            nc.vector.tensor_copy(dealt[:].rearrange("p (t m) -> p m t", t=PACK), src[:].rearrange("p (m t) -> p m t", t=PACK))
             return dealt
 
-        def pick(name, window, offsets, dtype, reuses=None):
-            picked = tile(name, [P, N], dtype, reuses)
+        def deal_pool(name, src, dtype):
+            dealt = tile(name, [P, N], dtype)
+            nc.gpsimd.tensor_copy(dealt[:].rearrange("p (t m) -> p t m", t=PACK), src[:].rearrange("p (m t) -> p t m", t=PACK))
+            return dealt
+
+        def pick(name, window, offsets, dtype):
+            picked = tile(name, [P, N], dtype)
             nc.vector.tensor_copy(picked[:], window[:].indirect(offsets[:]))
             return picked
 
@@ -107,43 +113,42 @@ def tile_picked_keymed_none_po_kernel(
                 stop=True,
             )
 
-        w2w_d = deal(nc.scalar.copy, "w2w_d", w2w, U32)
+        w2w_d = deal_vector("w2w_d", w2w, U32)
         x2s = pick("x2s", xs, two_l, U8)
         x1s = pick("x1s", xs, offs_l, U8)
         x2w = pick("x2w", xw, two_l, U32)
-        w2s_d = deal(nc.vector.tensor_copy, "w2s_d", w2s, U8)
+        w2s_d = deal_pool("w2s_d", w2s, U8)
         b_ps = [bank(f"b_ps{t}", N, PACK + t) for t in range(PACK)]
         for t in range(PACK):
             product(b_ps[t][:], w2w_d, w2s_d, t, x2w[:], x2s[:])
-        w1w_d = deal(nc.vector.tensor_copy, "w1w_d", w1w, U32)
-        x1w = pick("x1w", xw, offs_l, U32, reuses="w2s")
-        w1s_d = deal(nc.vector.tensor_copy, "w1s_d", w1s, U8)
+        w1w_d = deal_pool("w1w_d", w1w, U32)
+        x1w = pick("x1w", xw, offs_l, U32)
+        w1s_d = deal_pool("w1s_d", w1s, U8)
         a_ps = [bank(f"a_ps{t}", N, t) for t in range(PACK)]
         for t in range(PACK):
             product(a_ps[t][:], w1w_d, w1s_d, t, x1w[:], x1s[:])
 
-        def looked_up(window, held, h):
-            return window[:].indirect(held[:, h * (LIST_COLS // 2) : (h + 1) * (LIST_COLS // 2)])
+        def looked_up(window, held, c):
+            return window[:].indirect(held[:, c.start // 16 : c.stop // 16])
 
-        def fetch_scalar(out, window, held, h):
-            nc.scalar.activation(out, looked_up(window, held, h), ACT.Copy)
+        def fetch_scalar(out, window, held, c):
+            nc.scalar.activation(out, looked_up(window, held, c), ACT.Copy)
 
-        def fetch_vector(out, window, held, h):
-            nc.vector.tensor_copy(out, looked_up(window, held, h))
+        def fetch_vector(out, window, held, c):
+            nc.vector.tensor_copy(out, looked_up(window, held, c))
 
         def weave(copy, dst, src):
             copy(dst.rearrange("p (c i t) -> p c t i", i=4, t=PACK), src.rearrange("p t (c i) -> p c t i", i=4))
 
         sig_rows = [tile(f"sig_rows{t}", [P, N], F32) for t in range(PACK)]
-        gate = tile("gate", [P, PACK, N], F32, reuses="w1s")
         z2 = tile("z2", [P, PACK, N], BF16)
         z2_in = tile("z2_in", [P, PACK * N], BF16)
         z2w = tile("z2w", [P, N], U32)
         z2s = tile("z2s", [P, N], U8)
-        a_rows = [tile(f"a_rows{t}", [P, N], F32) for t in range(PACK)]
+        rows = [tile(f"rows{t}", [P, 2 * N], F32) for t in range(PACK)]
 
         def leave_a(t):
-            nc.scalar.activation(a_rows[t][:], a_ps[t][:], ACT.Copy, scale=ga_t[:, t : t + 1])
+            nc.scalar.activation(rows[t][:, :N], a_ps[t][:], ACT.Copy, scale=ga_t[:, t : t + 1])
 
         for t in range(PACK):
             nc.scalar.activation(sig_rows[t][:], b_ps[t][:], ACT.Sigmoid)
@@ -152,9 +157,9 @@ def tile_picked_keymed_none_po_kernel(
             for t in pair:
                 for h in range(2):
                     fetch = fetch_scalar if (t, h) == (PACK - 1, 1) else fetch_vector
-                    fetch(gate[:, t, cols(h)], sig_rows[t], nq_l, h)
+                    fetch(rows[t][:, N + h * HALF : N + (h + 1) * HALF], sig_rows[t], nq_l, cols(h))
             for t in pair:
-                nc.vector.scalar_tensor_tensor(z2[:, t, :], b_ps[t][:], gb_t[:, t : t + 1], gate[:, t, :], ALU.mult, ALU.mult)
+                nc.vector.scalar_tensor_tensor(z2[:, t, :], b_ps[t][:], gb_t[:, t : t + 1], rows[t][:, N:], ALU.mult, ALU.mult)
         weave(nc.vector.tensor_copy, z2_in[:], z2[:])
         nc.vector.quantize_mx(z2w[:].bitcast(FP8X4), z2s[:], z2_in[:])
 
@@ -174,27 +179,24 @@ def tile_picked_keymed_none_po_kernel(
         for t in range(PACK):
             if t > 0:
                 leave_a(t)
-            for h in range(2):
-                fetch_scalar(k1[:, t, cols(h)], a_rows[t], n1_l, h)
-                fetch_scalar(k2[:, t, cols(h)], a_rows[t], n2_l, h)
-            for c in [cols(0), cols(1)] if t == PACK - 1 else [slice(0, N)]:
+            for c in [cols(0), cols(1)] if t == PACK - 1 else [WHOLE]:
+                fetch_scalar(k1[:, t, c], rows[t], n1_l, c)
+                fetch_scalar(k2[:, t, c], rows[t], n2_l, c)
                 median(t, c)
 
         z_in = tile("z_in", [P, PACK, N], BF16)
         zw = tile("zw", [P, N], U32)
         zs = tile("zs", [P, N], U8)
         z_dealt = z[:].rearrange("p t (m u) -> p u m t", u=PACK)
-        s_ps = {}
+        s_ps = []
         for u in range(PACK):
             copy = nc.vector.tensor_copy if u < 2 else nc.scalar.copy
             copy(z_in[:, u, :].rearrange("p (m t) -> p m t", t=PACK), z_dealt[:, u])
             m = slice(u * P, (u + 1) * P)
             nc.vector.quantize_mx(zw[:, m].bitcast(FP8X4), zs[:, m], z_in[:, u, :])
-            for h in range(2):
-                s_ps[u, h] = bank(f"s_ps{u}{h}", HALF, (PACK + 2 * u + h) % BANKS)
-                product(s_ps[u, h][:], zw, zs, u, z2w[:, cols(h)], z2s[:, cols(h)])
+            s_ps.append(bank(f"s_ps{u}", N, PACK + u))
+            product(s_ps[u][:], zw, zs, u, z2w[:], z2s[:])
 
-        s_rows = [tile(f"s_rows{t}", [P, N], F32) for t in range(PACK)]
         got = tile("got", [P, PACK, N], F32)
         res = tile("res", [P, PACK, N], F32)
         res_in = tile("res_in", [P, PACK * N], BF16)
@@ -203,54 +205,37 @@ def tile_picked_keymed_none_po_kernel(
         out_rows = out_0.rearrange("(p t) v -> p t v", t=PACK)
         out_words = out_1[0].rearrange("p n t -> p (n t)").bitcast(I32)
 
-        def leave_s_scalar(t, h):
-            nc.scalar.activation(s_rows[t][:, cols(h)], s_ps[t, h][:], ACT.Copy, scale=-0.5 * S_SCALE)
+        def leave_s_scalar(t):
+            nc.scalar.activation(rows[t][:, :N], s_ps[t][:], ACT.Copy, scale=-0.5 * S_SCALE)
 
-        def leave_s_vector(t, h):
-            nc.vector.tensor_scalar(s_rows[t][:, cols(h)], s_ps[t, h][:], -0.5 * S_SCALE, None, ALU.mult)
+        def leave_s_vector(t):
+            nc.vector.tensor_scalar(rows[t][:, :N], s_ps[t][:], -0.5 * S_SCALE, None, ALU.mult)
 
-        def other_column(fetch, t, h):
-            fetch(got[:, t, cols(h)], s_rows[t], cq_l, h)
+        def other_column(fetch, t, c):
+            fetch(got[:, t, c], rows[t], cq_l, c)
 
-        def result(t, h):
-            nc.vector.scalar_tensor_tensor(res[:, t, cols(h)], s_ps[t, h][:], S_SCALE, got[:, t, cols(h)], ALU.mult, ALU.add)
+        def result(t):
+            nc.vector.scalar_tensor_tensor(res[:, t, :], s_ps[t][:], S_SCALE, got[:, t, :], ALU.mult, ALU.add)
+            nc.sync.dma_start(out_rows[:, t, :], res[:, t, :])
 
-        def store(ts, c):
-            nc.sync.dma_start(out_rows[:, ts, c], res[:, ts, c])
-
-        def planes(copy, h):
-            wide = slice(h * PACK * HALF, (h + 1) * PACK * HALF)
-            weave(copy, res_in[:, wide], res[:, :, cols(h)])
-            nc.vector.quantize_mx(out_w[:, cols(h)].bitcast(FP8X4), out_s[:, cols(h)], res_in[:, wide])
+        leave_s_vector(0)
+        leave_s_scalar(1)
+        other_column(fetch_vector, 0, WHOLE)
+        result(0)
+        other_column(fetch_scalar, 1, WHOLE)
+        leave_s_scalar(2)
+        leave_s_vector(3)
+        other_column(fetch_scalar, 2, WHOLE)
+        result(1)
+        other_column(fetch_vector, 3, cols(0))
+        other_column(fetch_scalar, 3, cols(1))
+        result(2)
+        result(3)
+        weave(nc.vector.tensor_copy, res_in[:, : PACK * WEAVE_CUT], res[:, :, :WEAVE_CUT])
+        weave(nc.scalar.copy, res_in[:, PACK * WEAVE_CUT :], res[:, :, WEAVE_CUT:])
+        for h in range(2):
+            nc.vector.quantize_mx(out_w[:, cols(h)].bitcast(FP8X4), out_s[:, cols(h)], res_in[:, h * PACK * HALF : (h + 1) * PACK * HALF])
             nc.sync.dma_start(out_words[:, cols(h)], out_w[:, cols(h)].bitcast(I32))
-
-        leave_s_vector(0, 0)
-        leave_s_scalar(0, 1)
-        for h in range(2):
-            leave_s_scalar(1, h)
-        for h in range(2):
-            other_column(fetch_vector, 0, h)
-        for h in range(2):
-            result(0, h)
-        store(slice(0, 1), slice(0, N))
-        for h in range(2):
-            other_column(fetch_scalar, 1, h)
-        for h in range(2):
-            leave_s_scalar(2, h)
-        for h in range(2):
-            leave_s_vector(3, h)
-        other_column(fetch_scalar, 2, 0)
-        other_column(fetch_vector, 3, 0)
-        other_column(fetch_scalar, 2, 1)
-        other_column(fetch_scalar, 3, 1)
-        for h in range(2):
-            result(1, h)
-        store(slice(1, 2), slice(0, N))
-        for h, copy in ((0, nc.scalar.copy), (1, nc.vector.tensor_copy)):
-            result(2, h)
-            result(3, h)
-            store(slice(2, PACK), cols(h))
-            planes(copy, h)
         for q in range(QUADRANTS):
             queue = nc.scalar if q % 2 else nc.sync
             queue.dma_start(out_2[0, 4 * q : 4 * q + 4, :].bitcast(I32), scale_rows(out_s, q))

from contextlib import ExitStack

import concourse.mybir as mybir

F32 = mybir.dt.float32
BF16 = mybir.dt.bfloat16
I32 = mybir.dt.int32
U32 = mybir.dt.uint32
U16 = mybir.dt.uint16
U8 = mybir.dt.uint8
FP8X4 = mybir.dt.float8_e4m3fn_x4
ALU = mybir.AluOpType
ACT = mybir.ActivationFunctionType

P = 128
PACK = 4
T = 2048
N = 512
HALF = N // 2
LIST_COLS = N // 16
QUADRANTS = 4
WHOLE = slice(0, N)
WEAVE_CUT = 320
S_SCALE = 0.0625
FLOPS = 3 * 2 * N * N * N


def tile_picked_keymed_none_po_kernel(
    tc, x_words, x_scales, w1_words, w1_scales, w2_words, w2_scales, ga, gb, offs, two, n1, n2, nq, cq, out_0, out_1, out_2
):
    nc = tc.nc
    with ExitStack() as ctx:
        lists = ctx.enter_context(tc.tile_pool(name="lists", bufs=1))
        sb = ctx.enter_context(tc.tile_pool(name="sb", bufs=1))
        psum = ctx.enter_context(tc.psum_pool(name="psum", bufs=1))

        def tile(name, shape, dtype):
            return sb.tile(shape, dtype, name=name, align_bytes=64)

        def bank(name, width, number):
            return psum.tile([P, width], F32, name=name, tag=f"bank{number}")

        def cols(h):
            return slice(h * HALF, (h + 1) * HALF)

        def scale_rows(held, q):
            return held[32 * q : 32 * q + 4, :].bitcast(I32)

        def load_list(name, src):
            held = lists.tile([P, LIST_COLS], U16, name=name)
            nc.sync.dma_start(held[:], src)
            return held

        def load_words(name, src, width):
            held = tile(name, [P, width], U32)
            nc.sync.dma_start(held[:].bitcast(I32), src[0].rearrange("p n t -> p (n t)").bitcast(I32))
            return held

        def load_scales(held, src):
            for q in range(QUADRANTS):
                nc.sync.dma_start(scale_rows(held, q), src[0, 4 * q : 4 * q + 4, :].bitcast(I32))

        def load_gain(name, src):
            held = tile(name, [P, PACK], F32)
            nc.sync.dma_start(held[:], src.rearrange("(p t) o -> p (t o)", t=PACK))
            return held

        xs = tile("xs", [P, T], U8)
        w2s = tile("w2s", [P, N], U8)
        w1s = tile("w1s", [P, N], U8)
        for held in (xs, w2s, w1s):
            nc.gpsimd.memset(held[:].bitcast(I32), 0)

        two_l = load_list("two_l", two)
        offs_l = load_list("offs_l", offs)
        w2w = load_words("w2w", w2_words, N)
        load_scales(xs, x_scales)
        xw = load_words("xw", x_words, T)
        load_scales(w2s, w2_scales)
        w1w = load_words("w1w", w1_words, N)
        nq_l = load_list("nq_l", nq)
        ga_t = load_gain("ga_t", ga)
        load_scales(w1s, w1_scales)
        n1_l = load_list("n1_l", n1)
        n2_l = load_list("n2_l", n2)
        gb_t = load_gain("gb_t", gb)
        cq_l = load_list("cq_l", cq)

        def deal_vector(name, src, dtype):
            dealt = tile(name, [P, N], dtype)
            nc.vector.tensor_copy(dealt[:].rearrange("p (t m) -> p m t", t=PACK), src[:].rearrange("p (m t) -> p m t", t=PACK))
            return dealt

        def deal_pool(name, src, dtype):
            dealt = tile(name, [P, N], dtype)
            nc.gpsimd.tensor_copy(dealt[:].rearrange("p (t m) -> p t m", t=PACK), src[:].rearrange("p (m t) -> p t m", t=PACK))
            return dealt

        def pick(name, window, offsets, dtype):
            picked = tile(name, [P, N], dtype)
            nc.vector.tensor_copy(picked[:], window[:].indirect(offsets[:]))
            return picked

        def product(out, dealt_words, dealt_scales, t, words, scales):
            m = slice(t * P, (t + 1) * P)
            nc.tensor.matmul_mx(
                out,
                lhsT=dealt_words[:, m].bitcast(FP8X4),
                lhsT_scale=dealt_scales[:, m],
                rhs=words.bitcast(FP8X4),
                rhs_scale=scales,
                start=True,
                stop=True,
            )

        w2w_d = deal_vector("w2w_d", w2w, U32)
        x2s = pick("x2s", xs, two_l, U8)
        x1s = pick("x1s", xs, offs_l, U8)
        x2w = pick("x2w", xw, two_l, U32)
        w2s_d = deal_pool("w2s_d", w2s, U8)
        b_ps = [bank(f"b_ps{t}", N, PACK + t) for t in range(PACK)]
        for t in range(PACK):
            product(b_ps[t][:], w2w_d, w2s_d, t, x2w[:], x2s[:])
        w1w_d = deal_pool("w1w_d", w1w, U32)
        x1w = pick("x1w", xw, offs_l, U32)
        w1s_d = deal_pool("w1s_d", w1s, U8)
        a_ps = [bank(f"a_ps{t}", N, t) for t in range(PACK)]
        for t in range(PACK):
            product(a_ps[t][:], w1w_d, w1s_d, t, x1w[:], x1s[:])

        def looked_up(window, held, c):
            return window[:].indirect(held[:, c.start // 16 : c.stop // 16])

        def fetch_scalar(out, window, held, c):
            nc.scalar.activation(out, looked_up(window, held, c), ACT.Copy)

        def fetch_vector(out, window, held, c):
            nc.vector.tensor_copy(out, looked_up(window, held, c))

        def weave(copy, dst, src):
            copy(dst.rearrange("p (c i t) -> p c t i", i=4, t=PACK), src.rearrange("p t (c i) -> p c t i", i=4))

        sig_rows = [tile(f"sig_rows{t}", [P, N], F32) for t in range(PACK)]
        z2 = tile("z2", [P, PACK, N], BF16)
        z2_in = tile("z2_in", [P, PACK * N], BF16)
        z2w = tile("z2w", [P, N], U32)
        z2s = tile("z2s", [P, N], U8)
        rows = [tile(f"rows{t}", [P, 2 * N], F32) for t in range(PACK)]

        def leave_a(t):
            nc.scalar.activation(rows[t][:, :N], a_ps[t][:], ACT.Copy, scale=ga_t[:, t : t + 1])

        for t in range(PACK):
            nc.scalar.activation(sig_rows[t][:], b_ps[t][:], ACT.Sigmoid)
        leave_a(0)
        for pair in ((0, 1), (2, 3)):
            for t in pair:
                for h in range(2):
                    fetch = fetch_scalar if (t, h) == (PACK - 1, 1) else fetch_vector
                    fetch(rows[t][:, N + h * HALF : N + (h + 1) * HALF], sig_rows[t], nq_l, cols(h))
            for t in pair:
                nc.vector.scalar_tensor_tensor(z2[:, t, :], b_ps[t][:], gb_t[:, t : t + 1], rows[t][:, N:], ALU.mult, ALU.mult)
        weave(nc.vector.tensor_copy, z2_in[:], z2[:])
        nc.vector.quantize_mx(z2w[:].bitcast(FP8X4), z2s[:], z2_in[:])

        k1 = tile("k1", [P, PACK, N], BF16)
        k2 = tile("k2", [P, PACK, N], BF16)
        lo = tile("lo", [P, PACK, N], BF16)
        hi = tile("hi", [P, PACK, N], BF16)
        mid = tile("mid", [P, PACK, N], BF16)
        z = tile("z", [P, PACK, N], BF16)

        def median(t, c):
            nc.vector.tensor_tensor(hi[:, t, c], k1[:, t, c], k2[:, t, c], ALU.max)
            nc.vector.tensor_tensor(lo[:, t, c], k1[:, t, c], k2[:, t, c], ALU.min)
            nc.vector.scalar_tensor_tensor(mid[:, t, c], a_ps[t][:, c], ga_t[:, t : t + 1], hi[:, t, c], ALU.mult, ALU.min)
            nc.vector.tensor_tensor(z[:, t, c], lo[:, t, c], mid[:, t, c], ALU.max)

        for t in range(PACK):
            if t > 0:
                leave_a(t)
            for c in [cols(0), cols(1)] if t == PACK - 1 else [WHOLE]:
                fetch_scalar(k1[:, t, c], rows[t], n1_l, c)
                fetch_scalar(k2[:, t, c], rows[t], n2_l, c)
                median(t, c)

        z_in = tile("z_in", [P, PACK, N], BF16)
        zw = tile("zw", [P, N], U32)
        zs = tile("zs", [P, N], U8)
        z_dealt = z[:].rearrange("p t (m u) -> p u m t", u=PACK)
        s_ps = []
        for u in range(PACK):
            copy = nc.vector.tensor_copy if u < 2 else nc.scalar.copy
            copy(z_in[:, u, :].rearrange("p (m t) -> p m t", t=PACK), z_dealt[:, u])
            m = slice(u * P, (u + 1) * P)
            nc.vector.quantize_mx(zw[:, m].bitcast(FP8X4), zs[:, m], z_in[:, u, :])
            s_ps.append(bank(f"s_ps{u}", N, PACK + u))
            product(s_ps[u][:], zw, zs, u, z2w[:], z2s[:])

        got = tile("got", [P, PACK, N], F32)
        res = tile("res", [P, PACK, N], F32)
        res_in = tile("res_in", [P, PACK * N], BF16)
        out_w = tile("out_w", [P, N], U32)
        out_s = tile("out_s", [P, N], U8)
        out_rows = out_0.rearrange("(p t) v -> p t v", t=PACK)
        out_words = out_1[0].rearrange("p n t -> p (n t)").bitcast(I32)

        def leave_s_scalar(t):
            nc.scalar.activation(rows[t][:, :N], s_ps[t][:], ACT.Copy, scale=-0.5 * S_SCALE)

        def leave_s_vector(t):
            nc.vector.tensor_scalar(rows[t][:, :N], s_ps[t][:], -0.5 * S_SCALE, None, ALU.mult)

        def other_column(fetch, t, c):
            fetch(got[:, t, c], rows[t], cq_l, c)

        def result(t):
            nc.vector.scalar_tensor_tensor(res[:, t, :], s_ps[t][:], S_SCALE, got[:, t, :], ALU.mult, ALU.add)
            nc.sync.dma_start(out_rows[:, t, :], res[:, t, :])

        leave_s_vector(0)
        leave_s_scalar(1)
        other_column(fetch_vector, 0, WHOLE)
        result(0)
        other_column(fetch_scalar, 1, WHOLE)
        leave_s_scalar(2)
        leave_s_vector(3)
        other_column(fetch_scalar, 2, WHOLE)
        result(1)
        other_column(fetch_vector, 3, cols(0))
        other_column(fetch_scalar, 3, cols(1))
        result(2)
        result(3)
        weave(nc.vector.tensor_copy, res_in[:, : PACK * WEAVE_CUT], res[:, :, :WEAVE_CUT])
        weave(nc.scalar.copy, res_in[:, PACK * WEAVE_CUT :], res[:, :, WEAVE_CUT:])
        for h in range(2):
            nc.vector.quantize_mx(out_w[:, cols(h)].bitcast(FP8X4), out_s[:, cols(h)], res_in[:, h * PACK * HALF : (h + 1) * PACK * HALF])
            nc.sync.dma_start(out_words[:, cols(h)], out_w[:, cols(h)].bitcast(I32))
        for q in range(QUADRANTS):
            queue = nc.scalar if q % 2 else nc.sync
            queue.dma_start(out_2[0, 4 * q : 4 * q + 4, :].bitcast(I32), scale_rows(out_s, q))
